import numpy as np
import ml_dtypes


def mxq(x, axis, fmt="e4m3"):
    dtype, down = {"e4m3": (ml_dtypes.float8_e4m3fn, 7), "e5m2": (ml_dtypes.float8_e5m2, 14)}[fmt]
    v = np.moveaxis(np.asarray(x, np.float32).astype(ml_dtypes.bfloat16).astype(np.float64), axis, -1)
    blocks = v.reshape(v.shape[:-1] + (-1, 32))
    amax = np.abs(blocks).max(-1, keepdims=True)
    byte = np.maximum(np.where(amax > 0, np.frexp(amax)[1] - 1 + 127, 0) - down, 1)
    scale = np.exp2(byte - 127.0)
    codes = (blocks / scale).astype(np.float32).astype(dtype).astype(np.float64)
    return np.moveaxis((codes * scale).reshape(v.shape), -1, axis)


WIDE = False


def mx_kscale(k):
    if not WIDE:
        return np.ones(k)
    levels = np.array([10, -10, 5, -5, 0])
    if k % 512:
        return np.exp2(np.random.permutation(np.resize(levels, k // 32))).repeat(32)
    a = np.empty((k // 512, 16))
    for p in range(k // 512):
        a[p, :8] = np.random.permutation(np.resize(levels, 8))
        for g in range(8):
            far = levels[np.abs(levels - a[p, g]) >= 10]
            a[p, g + 8] = far[np.random.randint(len(far))]
    return np.exp2(a.ravel()).repeat(32)


BF16 = ml_dtypes.bfloat16


def bf(x):
    return np.asarray(x, np.float32).astype(BF16)


def f64(x):
    return np.asarray(x).astype(np.float64)


E2M1 = np.array([0.0, 0.5, 1.0, 1.5, 2.0, 3.0, 4.0, 6.0, -0.0, -0.5, -1.0, -1.5, -2.0, -3.0, -4.0, -6.0])


def pack_weight(w, fmt):
    k, n = w.shape
    w = f64(bf(w)).reshape(k // 32, 32, n)
    amax = np.abs(w).max(1)
    if fmt == "e4m3":
        byte = np.frexp(amax)[1] - 1 + 127 - 7
    else:
        mant, ex = np.frexp(amax / 6.0)
        byte = np.where(mant > 0.5, ex, ex - 1) + 127
    byte = np.clip(np.where(amax > 0, byte, 1), 1, 254)
    scaled = (w * np.exp2(127.0 - byte)[:, None, :]).reshape(k, n).astype(np.float32)
    by_word = np.ascontiguousarray(scaled.reshape(k // 512, 128, 4, n).transpose(0, 1, 3, 2))
    if fmt == "e4m3":
        words = by_word.astype(ml_dtypes.float8_e4m3fn).view(np.uint8)
    else:
        c = by_word.astype(ml_dtypes.float4_e2m1fn).view(np.uint8) & 0xF
        words = c[..., 0::2] | (c[..., 1::2] << 4)
    return np.ascontiguousarray(words), np.ascontiguousarray(byte.astype(np.uint8).reshape(k // 512, 16, n))


def unpack_weight(words, scales, fmt):
    g, p, n, _ = words.shape
    if fmt == "e4m3":
        vals = np.ascontiguousarray(words).view(ml_dtypes.float8_e4m3fn).astype(np.float64)
    else:
        nib = np.empty((g, p, n, 4), np.uint8)
        nib[..., 0::2] = words & 0xF
        nib[..., 1::2] = words >> 4
        vals = E2M1[nib]
    vals = vals * np.repeat(np.exp2(scales.astype(np.float64) - 127.0), 8, axis=1)[..., None]
    return vals.transpose(0, 1, 3, 2).reshape(g * 512, n)
def pack4(w):
    words, scales = pack_weight(w, "e2m1")
    return words.reshape(words.shape[0], 128, -1), scales


def unpack4(words, scales):
    return unpack_weight(words.reshape(words.shape[0], 128, -1, 2), scales, "e2m1")


P, T, D, H, S = 8, 2048, 1024, 1024, 1536


def setup_inputs():
    s = mx_kscale(D)
    u = mx_kscale(T)
    x = np.random.standard_normal((T, D)) * s * u[:, None]
    w = np.random.standard_normal((D, H)) / np.sqrt(D) / s[:, None]
    lhuc = np.random.standard_normal((P, H))
    err = np.random.standard_normal((T, S)) / np.sqrt(T) / u[:, None]
    err_words, err_scales = pack4(err)
    return {"x": bf(x),
            "w": bf(w),
            "lhuc": bf(lhuc),
            "err_words": err_words,
            "err_scales": err_scales}


def reference(x, w, lhuc, err_words, err_scales):
    z = mxq(f64(x), 1, "e4m3") @ mxq(f64(w), 0, "e4m3")
    amp = 2.0 / (1.0 + np.exp(-f64(lhuc)))
    h = np.maximum(z, 0.0).reshape(P, T // P, H) * amp[:, None, :]
    h = h.reshape(T, H)
    e = unpack4(err_words, err_scales)
    return mxq(h, 0, "e4m3").T @ e

@@ -1,0 +1,358 @@
+from contextlib import ExitStack
+
+from concourse.masks import make_identity
+import concourse.mybir as mybir
+
+F32 = mybir.dt.float32
+BF16 = mybir.dt.bfloat16
+I32 = mybir.dt.int32
+U32 = mybir.dt.uint32
+U8 = mybir.dt.uint8
+FP8X4 = mybir.dt.float8_e4m3fn_x4
+FP4X4 = mybir.dt.float4_e2m1fn_x4
+ALU = mybir.AluOpType
+ACT = mybir.ActivationFunctionType
+
+T, D, H, S, SPK = 2048, 1024, 1024, 1536, 8
+P = 128
+G = T // 512
+Q = D // 512
+NH = H // P
+NS = S // 512
+WC = 256
+
+FLOPS = 2 * T * D * H + 2 * T * H * S
+BYTES = 2 * T * D + 2 * D * H + 2 * SPK * H + T * S // 2 + T * S // 32 + 4 * H * S
+
+
+def tile_lhuc_senone_gradient_s13_kernel(tc, x, w, lhuc, err_words, err_scales, out):
+    nc = tc.nc
+    with ExitStack() as ctx:
+        keep = ctx.enter_context(tc.tile_pool(name="keep", bufs=1))
+        work = ctx.enter_context(tc.tile_pool(name="work", bufs=4))
+        psum = ctx.enter_context(tc.psum_pool(name="psum", bufs=1))
+
+        ident = keep.tile([P, P], F32, name="ident")
+        dummy = keep.tile([P, 1], F32, name="dummy")
+        xraw = [keep.tile([P, 4, D], BF16, name="xraw%d" % g) for g in range(G)]
+        xcod = [keep.tile([P, 4, Q * P], U32, name="xcod%d" % g, align_bytes=64) for g in range(G)]
+        xsca = [keep.tile([P, 4, Q * P], U8, name="xsca%d" % g, align_bytes=64) for g in range(G)]
+        wraw = [[keep.tile([P, 4, WC], BF16, name="wraw%d_%d" % (c, q)) for q in range(Q)] for c in range(H // WC)]
+        wcod = [[keep.tile([P, WC], U32, name="wcod%d_%d" % (c, q), align_bytes=64) for q in range(Q)] for c in range(H // WC)]
+        wsca = [[keep.tile([P, WC], U8, name="wsca%d_%d" % (c, q), align_bytes=64) for q in range(Q)] for c in range(H // WC)]
+        lraw = [keep.tile([P, G, 512], BF16, name="lraw%d" % c) for c in range(2)]
+        amp = [keep.tile([P, G, 512], F32, name="amp%d" % c) for c in range(2)]
+        hcod = [keep.tile([P, G, P], U32, name="hcod%d" % h, align_bytes=64) for h in range(NH)]
+        hsca = [keep.tile([P, G, P], U8, name="hsca%d" % h, align_bytes=64) for h in range(NH)]
+        ewor = [keep.tile([P, 2 * S], U8, name="ewor%d" % g, align_bytes=64) for g in range(G)]
+        esca = keep.tile([P, G, S], U8, name="esca", align_bytes=64)
+
+        def bank(i):
+            b = psum.tile([P, 512], F32, name="bank%d" % i, tag="bank%d" % i)
+            return b
+
+        xbanks = [0, 1, 2, 3]
+        zbanks = [4, 5, 6]
+        obanks = [7, 2, 0, 3, 1]
+        count = {"z": 0, "o": 0}
+
+        def load_x(g, a, b):
+            nc.sync.dma_start(out=xraw[g][:, a:b, :], in_=x[512 * g : 512 * (g + 1), :].rearrange("(m t) k -> m t k", t=4)[:, a:b, :])
+
+        def load_w(c):
+            for q in range(Q):
+                nc.sync.dma_start(
+                    out=wraw[c][q][:],
+                    in_=w[512 * q : 512 * (q + 1), WC * c : WC * (c + 1)].rearrange("(p j) n -> p j n", j=4),
+                )
+
+        def load_lhuc(c, lo, hi):
+            rows = lhuc.rearrange("(g s) n -> s g n", s=2)
+            for s in range(2):
+                nc.sync.dma_start(
+                    out=lraw[c][64 * s : 64 * (s + 1), lo:hi, :],
+                    in_=rows[s, lo:hi, 512 * c : 512 * (c + 1)].partition_broadcast(64),
+                )
+
+        def load_esca():
+            for k in range(4):
+                nc.sync.dma_start(
+                    out=esca[32 * k : 32 * k + 4, :, :].bitcast(I32),
+                    in_=err_scales[:, 4 * k : 4 * (k + 1), :].rearrange("g r n -> r g n").bitcast(I32),
+                )
+
+        def load_ewor(g):
+            nc.sync.dma_start(out=ewor[g][:].bitcast(I32), in_=err_words[g].bitcast(I32))
+
+        xgrp = {}
+        xord = {}
+
+        def xorder(g, t, eng):
+            xo = work.tile([P, 512], F32, name="xo", tag="xo", bufs=6)
+            dst = xo[:].rearrange("p (q u m) -> p q u m", q=Q, u=2)
+            src = xraw[g][:, t, :].bitcast(F32).rearrange("p (q m u) -> p q u m", q=Q, u=2)
+            if eng == "s":
+                nc.scalar.copy(out=dst, in_=src)
+            else:
+                nc.vector.tensor_copy(out=dst, in_=src)
+            xord[g, t] = xo
+
+        def trans(g, t):
+            b = bank(xbanks[t])
+            words = xraw[g][:, t, :].bitcast(F32)
+            for q in range(Q):
+                for u in range(2):
+                    j = 2 * q + u
+                    if (g, t) in xord:
+                        cols = xord[g, t][:, P * j : P * (j + 1)]
+                    else:
+                        cols = words[:, 256 * q + u : 256 * (q + 1) : 2]
+                    nc.tensor.transpose(b[:, P * j : P * (j + 1)], cols, ident[:])
+            xg = work.tile([P, Q, P, 4], BF16, name="xg", tag="xg", align_bytes=64)
+            nc.scalar.copy(
+                out=xg[:].rearrange("p q m t -> p (q m t)").bitcast(F32),
+                in_=b[:].rearrange("p (q u m) -> p q m u", q=Q, u=2),
+            )
+            xgrp[g, t] = xg
+
+        def xquant(g, t):
+            nc.vector.quantize_mx(
+                out=xcod[g][:, t, :].bitcast(FP8X4),
+                scales=xsca[g][:, t, :],
+                in_=xgrp[g, t][:].rearrange("p q m t -> p (q m t)"),
+            )
+
+        wgrp = {}
+
+        def winter(h, q, eng, n=1):
+            c, off = divmod(P * h, WC)
+            wg = work.tile([P, P * n, 4], BF16, name="wg", tag="wg", align_bytes=64)
+            src = wraw[c][q][:, :, off : off + P * n].rearrange("p j n -> p n j")
+            if eng == "s":
+                nc.scalar.copy(out=wg[:], in_=src)
+            else:
+                nc.vector.tensor_copy(out=wg[:], in_=src)
+            wgrp[h, q] = wg
+
+        def wquant(h, q, n=1):
+            c, off = divmod(P * h, WC)
+            nc.vector.quantize_mx(
+                out=wcod[c][q][:, off : off + P * n].bitcast(FP8X4),
+                scales=wsca[c][q][:, off : off + P * n],
+                in_=wgrp[h, q][:].rearrange("p n j -> p (n j)"),
+            )
+
+        def sigm(c, lo, hi):
+            nc.scalar.activation(out=amp[c][:, lo:hi, :], in_=lraw[c][:, lo:hi, :], func=ACT.Sigmoid)
+
+        zb = {}
+        hgrp = {}
+
+        def s1(g, h):
+            z = bank(zbanks[count["z"] % len(zbanks)])
+            count["z"] += 1
+            c, off = divmod(P * h, WC)
+            for t in range(4):
+                for q in range(Q):
+                    nc.tensor.matmul_mx(
+                        out=z[:, P * t : P * (t + 1)],
+                        lhsT=xcod[g][:, t, P * q : P * (q + 1)].bitcast(FP8X4),
+                        lhsT_scale=xsca[g][:, t, P * q : P * (q + 1)],
+                        rhs=wcod[c][q][:, off : off + P].bitcast(FP8X4),
+                        rhs_scale=wsca[c][q][:, off : off + P],
+                        start=(q == 0),
+                        stop=(q == Q - 1),
+                    )
+            zb[g, h] = z
+
+        def hevict(g, h):
+            c, off = divmod(P * h, 512)
+            hg = work.tile([P, P, 4], BF16, name="hg", tag="hg", align_bytes=64)
+            nc.vector.scalar_tensor_tensor(
+                out=hg[:],
+                in0=zb[g, h][:].rearrange("p (t n) -> p n t", t=4),
+                scalar=0.0,
+                in1=amp[c][:, g, off : off + P].unsqueeze(2).to_broadcast([P, P, 4]),
+                op0=ALU.max,
+                op1=ALU.mult,
+            )
+            hgrp[g, h] = hg
+
+        def hquant(g, h):
+            nc.vector.quantize_mx(
+                out=hcod[h][:, g, :].bitcast(FP8X4),
+                scales=hsca[h][:, g, :],
+                in_=hgrp[g, h][:].rearrange("p n t -> p (n t)"),
+            )
+
+        pend = []
+
+        def s1h(g, h):
+            s1(g, h)
+            hevict(g, h)
+            if pend:
+                hquant(*pend.pop())
+            pend.append((g, h))
+
+        def flush():
+            if pend:
+                hquant(*pend.pop())
+
+        ob = {}
+        og = {}
+
+        def s2(h, n, groups):
+            if groups[0] == 0:
+                ob[h, n] = bank(obanks[count["o"] % len(obanks)])
+                count["o"] += 1
+            for g in groups:
+                nc.tensor.matmul_mx(
+                    out=ob[h, n][:],
+                    lhsT=hcod[h][:, g, :].bitcast(FP8X4),
+                    lhsT_scale=hsca[h][:, g, :],
+                    rhs=ewor[g][:, 1024 * n : 1024 * (n + 1)].bitcast(FP4X4),
+                    rhs_scale=esca[:, g, 512 * n : 512 * (n + 1)],
+                    start=(g == 0),
+                    stop=(g == G - 1),
+                )
+
+        def oevict(h, n, eng, lo=0, hi=512):
+            if h not in og:
+                og[h] = work.tile([P, S], F32, name="og", tag="og", bufs=3)
+            dst = og[h][:, 512 * n + lo : 512 * n + hi]
+            src = ob[h, n][:, lo:hi]
+            if eng == "s":
+                nc.scalar.activation(out=dst, in_=src, func=ACT.Copy, scale=2.0)
+            else:
+                nc.vector.tensor_scalar(out=dst, in0=src, scalar1=2.0, scalar2=None, op0=ALU.mult)
+
+        def store(h, lo, hi):
+            nc.sync.dma_start(out=out[P * h : P * (h + 1), lo:hi], in_=og[h][:, lo:hi])
+
+        with tc.manual_schedule():
+            nc.vector.memset(dummy[:], 0.0)
+            nc.scalar.activation(out=dummy[:], in_=dummy[:], func=ACT.Sigmoid)
+            make_identity(nc, ident[:])
+            nc.vector.memset(esca[:].rearrange("p g n -> p (g n)").bitcast(I32), 0)
+            load_x(0, 0, 1)
+            load_x(0, 1, 2)
+            load_x(0, 2, 3)
+            load_x(0, 3, 4)
+            load_w(0)
+            load_lhuc(0, 0, 1)
+            load_x(1, 0, 2)
+            load_x(1, 2, 4)
+            load_w(1)
+            load_lhuc(0, 1, 4)
+            load_x(2, 0, 4)
+            load_x(3, 0, 4)
+            load_esca()
+            for g in range(G):
+                load_ewor(g)
+            load_w(2)
+            load_lhuc(1, 0, 4)
+            load_w(3)
+
+            for t in range(4):
+                trans(0, t)
+            xquant(0, 0)
+            xquant(0, 1)
+            winter(0, 0, "v")
+            winter(0, 1, "v")
+            xquant(0, 2)
+            wquant(0, 0)
+            wquant(0, 1)
+            xquant(0, 3)
+            winter(1, 1, "s")
+            winter(1, 0, "v")
+            sigm(0, 0, 1)
+            wquant(1, 1)
+            wquant(1, 0)
+            s1h(0, 0)
+            s1h(0, 1)
+            flush()
+            trans(1, 0)
+            winter(2, 0, "v")
+            xquant(1, 0)
+            trans(1, 1)
+            winter(2, 1, "v")
+            wquant(2, 0)
+            xquant(1, 1)
+            wquant(2, 1)
+            trans(1, 2)
+            xquant(1, 2)
+            trans(1, 3)
+            winter(3, 0, "v")
+            xquant(1, 3)
+            winter(3, 1, "s")
+            s1h(0, 2)
+            sigm(0, 1, 2)
+            wquant(3, 0)
+            wquant(3, 1)
+            s1h(1, 0)
+            s1h(1, 1)
+            xorder(2, 0, "s")
+            xorder(2, 1, "s")
+            s1h(0, 3)
+            for t in (2, 3, 0, 1):
+                trans(2, t)
+                xquant(2, t)
+            xorder(3, 0, "s")
+            xorder(3, 1, "s")
+            xorder(3, 2, "v")
+            xorder(3, 3, "v")
+            s1h(1, 2)
+            s1h(1, 3)
+            for t in (2, 0, 3, 1):
+                trans(3, t)
+                xquant(3, t)
+            sigm(0, 2, 4)
+            s1h(2, 0)
+            s1h(2, 1)
+            for n in range(NS):
+                s2(0, n, [0])
+            s1h(2, 2)
+            for n in range(NS):
+                s2(0, n, [1])
+            winter(4, 0, "s", 2)
+            s1h(2, 3)
+            s1h(3, 0)
+            winter(4, 1, "s", 2)
+            s1h(3, 1)
+            wquant(4, 0, 2)
+            for n in range(NS):
+                s2(0, n, [2])
+            sigm(1, 0, 4)
+            s1h(3, 2)
+            wquant(4, 1, 2)
+            for n in range(NS):
+                s2(0, n, [3])
+                oevict(0, n, "s")
+            store(0, 0, S)
+            s1h(3, 3)
+            winter(6, 0, "s", 2)
+            winter(6, 1, "s", 2)
+            for h in range(1, NH):
+                z = h + 3
+                if z < NH:
+                    s1h(0, z)
+                if h == 1:
+                    wquant(6, 0, 2)
+                    wquant(6, 1, 2)
+                for n in range(NS):
+                    s2(h, n, [0, 1, 2, 3])
+                    if h < NH - 1:
+                        oevict(h, n, "s")
+                    elif n < NS - 1:
+                        oevict(h, n, "sv"[n])
+                        store(h, 512 * n, 512 * (n + 1))
+                    else:
+                        oevict(h, n, "s", 0, 256)
+                        oevict(h, n, "v", 256, 512)
+                        store(h, 512 * n, 512 * (n + 1))
+                    if z < NH:
+                        s1h(n + 1, z)
+                if h < NH - 1:
+                    store(h, 0, S)
+                if z == NH - 1:
+                    flush()

@@ -33,6 +33,10 @@ def tile_lhuc_senone_gradient_s13_kernel(tc, x, w, lhuc, err_words, err_scales, 
         psum = ctx.enter_context(tc.psum_pool(name="psum", bufs=1))
 
         ident = keep.tile([P, P], F32, name="ident")
+        identb = keep.tile([P, P], BF16, name="identb")
+        lrow = keep.tile([P, 512], BF16, name="lrow", align_bytes=64)
+        lcol = keep.tile([P, 4, SPK], BF16, name="lcol", align_bytes=64)
+        lrep = keep.tile([P, 2, G, 2, 2, 64], BF16, name="lrep", align_bytes=64)
         dummy = keep.tile([P, 1], F32, name="dummy")
         xraw = [keep.tile([P, 4, D], BF16, name="xraw%d" % g) for g in range(G)]
         xcod = [keep.tile([P, 4, Q * P], U32, name="xcod%d" % g, align_bytes=64) for g in range(G)]
@@ -41,7 +45,7 @@ def tile_lhuc_senone_gradient_s13_kernel(tc, x, w, lhuc, err_words, err_scales, 
         wcod = [[keep.tile([P, WC], U32, name="wcod%d_%d" % (c, q), align_bytes=64) for q in range(Q)] for c in range(H // WC)]
         wsca = [[keep.tile([P, WC], U8, name="wsca%d_%d" % (c, q), align_bytes=64) for q in range(Q)] for c in range(H // WC)]
         lraw = [keep.tile([P, G, 512], BF16, name="lraw%d" % c) for c in range(2)]
-        amp = [keep.tile([P, G, 512], F32, name="amp%d" % c) for c in range(2)]
+        amp = [keep.tile([P, G, 256], F32, name="amp%d" % c) for c in range(4)]
         hcod = [keep.tile([P, G, P], U32, name="hcod%d" % h, align_bytes=64) for h in range(NH)]
         hsca = [keep.tile([P, G, P], U8, name="hsca%d" % h, align_bytes=64) for h in range(NH)]
         ewor = [keep.tile([P, 2 * S], U8, name="ewor%d" % g, align_bytes=64) for g in range(G)]
@@ -53,7 +57,7 @@ def tile_lhuc_senone_gradient_s13_kernel(tc, x, w, lhuc, err_words, err_scales, 
 
         xbanks = [0, 1, 2, 3]
         zbanks = [4, 5, 6]
-        obanks = [7, 2, 0, 3, 1]
+        obanks = [7, 1, 0, 3, 2]
         count = {"z": 0, "o": 0}
 
         def load_x(g, a, b):
@@ -142,8 +146,30 @@ def tile_lhuc_senone_gradient_s13_kernel(tc, x, w, lhuc, err_words, err_scales, 
                 in_=wgrp[h, q][:].rearrange("p n j -> p (n j)"),
             )
 
+        def lhuc_turn():
+            b = psum.tile([P, 4, P], BF16, name="bank5l", tag="bank5")
+            for h in range(4):
+                nc.tensor.transpose(b[:, h, :], lrow[:, P * h : P * (h + 1)], identb[:])
+            nc.vector.tensor_copy(out=lcol[:], in_=b[:, :, 0:SPK])
+
+        def lhuc_repeat(a, g, eng):
+            src = lcol[:, 2 * a : 2 * (a + 1), 2 * g : 2 * (g + 1)].unsqueeze(3).to_broadcast([P, 2, 2, 64])
+            if eng == "s":
+                nc.scalar.copy(out=lrep[:, a, g, :, :, :], in_=src)
+            else:
+                nc.vector.tensor_copy(out=lrep[:, a, g, :, :, :], in_=src)
+
+        def lhuc_spread(a, lo, hi, i):
+            b = psum.tile([P, G, 256], BF16, name="bank%dl" % i, tag="bank%d" % i)
+            for g in range(lo, hi):
+                for h in range(2):
+                    nc.tensor.transpose(
+                        b[:, g, P * h : P * (h + 1)], lrep[:, a, g, h, :, :].rearrange("p s r -> p (s r)"), identb[:]
+                    )
+            nc.scalar.activation(out=amp[a][:, lo:hi, :], in_=b[:, lo:hi, :], func=ACT.Sigmoid)
+
         def sigm(c, lo, hi):
-            nc.scalar.activation(out=amp[c][:, lo:hi, :], in_=lraw[c][:, lo:hi, :], func=ACT.Sigmoid)
+            nc.scalar.activation(out=amp[c][:, lo:hi, :], in_=lraw[c // 2][:, lo:hi, 256 * (c % 2) : 256 * (c % 2 + 1)], func=ACT.Sigmoid)
 
         zb = {}
         hgrp = {}
@@ -166,7 +192,7 @@ def tile_lhuc_senone_gradient_s13_kernel(tc, x, w, lhuc, err_words, err_scales, 
             zb[g, h] = z
 
         def hevict(g, h):
-            c, off = divmod(P * h, 512)
+            c, off = divmod(P * h, 256)
             hg = work.tile([P, P, 4], BF16, name="hg", tag="hg", align_bytes=64)
             nc.vector.scalar_tensor_tensor(
                 out=hg[:],
@@ -231,30 +257,35 @@ def tile_lhuc_senone_gradient_s13_kernel(tc, x, w, lhuc, err_words, err_scales, 
 
         with tc.manual_schedule():
             nc.vector.memset(dummy[:], 0.0)
+            nc.vector.memset(lrow[:], 0.0)
+            nc.scalar.dma_start(out=lrow[0:SPK, :], in_=lhuc[:, 0:512])
             nc.scalar.activation(out=dummy[:], in_=dummy[:], func=ACT.Sigmoid)
             make_identity(nc, ident[:])
+            make_identity(nc, identb[:])
             nc.vector.memset(esca[:].rearrange("p g n -> p (g n)").bitcast(I32), 0)
             load_x(0, 0, 1)
             load_x(0, 1, 2)
             load_x(0, 2, 3)
             load_x(0, 3, 4)
             load_w(0)
-            load_lhuc(0, 0, 1)
             load_x(1, 0, 2)
             load_x(1, 2, 4)
-            load_w(1)
-            load_lhuc(0, 1, 4)
             load_x(2, 0, 4)
             load_x(3, 0, 4)
+            load_w(1)
             load_esca()
             for g in range(G):
                 load_ewor(g)
             load_w(2)
-            load_lhuc(1, 0, 4)
             load_w(3)
+            load_lhuc(1, 0, 4)
 
-            for t in range(4):
-                trans(0, t)
+            trans(0, 0)
+            trans(0, 1)
+            lhuc_turn()
+            lhuc_repeat(0, 0, "v")
+            trans(0, 2)
+            trans(0, 3)
             xquant(0, 0)
             xquant(0, 1)
             winter(0, 0, "v")
@@ -263,84 +294,77 @@ def tile_lhuc_senone_gradient_s13_kernel(tc, x, w, lhuc, err_words, err_scales, 
             wquant(0, 0)
             wquant(0, 1)
             xquant(0, 3)
-            winter(1, 1, "s")
-            winter(1, 0, "v")
-            sigm(0, 0, 1)
+            lhuc_spread(0, 0, 1, 7)
+            winter(1, 0, "s")
+            winter(1, 1, "v")
+            lhuc_repeat(0, 1, "v")
             wquant(1, 1)
             wquant(1, 0)
+            lhuc_repeat(0, 2, "v")
+            lhuc_repeat(0, 3, "v")
             s1h(0, 0)
-            s1h(0, 1)
-            flush()
             trans(1, 0)
-            winter(2, 0, "v")
             xquant(1, 0)
             trans(1, 1)
-            winter(2, 1, "v")
-            wquant(2, 0)
             xquant(1, 1)
-            wquant(2, 1)
+            xorder(2, 0, "v")
             trans(1, 2)
             xquant(1, 2)
+            xorder(2, 1, "v")
             trans(1, 3)
-            winter(3, 0, "v")
             xquant(1, 3)
-            winter(3, 1, "s")
-            s1h(0, 2)
-            sigm(0, 1, 2)
-            wquant(3, 0)
-            wquant(3, 1)
-            s1h(1, 0)
-            s1h(1, 1)
-            xorder(2, 0, "s")
-            xorder(2, 1, "s")
-            s1h(0, 3)
-            for t in (2, 3, 0, 1):
+            xorder(2, 2, "v")
+            xorder(2, 3, "v")
+            lhuc_spread(0, 1, 4, 6)
+            s1h(0, 1)
+            for t in range(4):
                 trans(2, t)
                 xquant(2, t)
+                if t % 2:
+                    xorder(3, t, "v")
             xorder(3, 0, "s")
-            xorder(3, 1, "s")
-            xorder(3, 2, "v")
-            xorder(3, 3, "v")
-            s1h(1, 2)
-            s1h(1, 3)
-            for t in (2, 0, 3, 1):
+            s1h(1, 0)
+            s1h(1, 1)
+            for t in (1, 0, 3, 2):
                 trans(3, t)
                 xquant(3, t)
-            sigm(0, 2, 4)
             s1h(2, 0)
+            winter(2, 0, "s")
             s1h(2, 1)
-            for n in range(NS):
-                s2(0, n, [0])
-            s1h(2, 2)
-            for n in range(NS):
-                s2(0, n, [1])
-            winter(4, 0, "s", 2)
-            s1h(2, 3)
+            for g in (0, 1):
+                for n in range(NS):
+                    s2(0, n, [g])
+            winter(2, 1, "s")
+            for g in range(G):
+                lhuc_repeat(1, g, "s")
+            wquant(2, 0)
+            wquant(2, 1)
             s1h(3, 0)
-            winter(4, 1, "s", 2)
             s1h(3, 1)
-            wquant(4, 0, 2)
-            for n in range(NS):
-                s2(0, n, [2])
-            sigm(1, 0, 4)
-            s1h(3, 2)
-            wquant(4, 1, 2)
-            for n in range(NS):
-                s2(0, n, [3])
-                oevict(0, n, "s")
-            store(0, 0, S)
-            s1h(3, 3)
-            winter(6, 0, "s", 2)
-            winter(6, 1, "s", 2)
-            for h in range(1, NH):
-                z = h + 3
+            flush()
+            lhuc_spread(1, 0, 4, 3)
+            winter(3, 0, "s")
+            winter(3, 1, "v")
+            wquant(3, 0)
+            wquant(3, 1)
+            for h in range(NH):
+                z = h + 2
                 if z < NH:
                     s1h(0, z)
-                if h == 1:
+                if z == 3:
+                    winter(4, 0, "s", 2)
+                    winter(4, 1, "s", 2)
+                    sigm(2, 0, 4)
+                    wquant(4, 0, 2)
+                    wquant(4, 1, 2)
+                if z == 5:
+                    sigm(3, 0, 4)
+                    winter(6, 0, "s", 2)
+                    winter(6, 1, "s", 2)
                     wquant(6, 0, 2)
                     wquant(6, 1, 2)
                 for n in range(NS):
-                    s2(h, n, [0, 1, 2, 3])
+                    s2(h, n, [2, 3] if h == 0 else [0, 1, 2, 3])
                     if h < NH - 1:
                         oevict(h, n, "s")
                     elif n < NS - 1:

from contextlib import ExitStack

from concourse.masks import make_identity
import concourse.mybir as mybir

F32 = mybir.dt.float32
BF16 = mybir.dt.bfloat16
I32 = mybir.dt.int32
U32 = mybir.dt.uint32
U8 = mybir.dt.uint8
FP8X4 = mybir.dt.float8_e4m3fn_x4
FP4X4 = mybir.dt.float4_e2m1fn_x4
ALU = mybir.AluOpType
ACT = mybir.ActivationFunctionType

T, D, H, S, SPK = 2048, 1024, 1024, 1536, 8
P = 128
G = T // 512
Q = D // 512
NH = H // P
NS = S // 512
WC = 256

FLOPS = 2 * T * D * H + 2 * T * H * S
BYTES = 2 * T * D + 2 * D * H + 2 * SPK * H + T * S // 2 + T * S // 32 + 4 * H * S


def tile_lhuc_senone_gradient_s13_kernel(tc, x, w, lhuc, err_words, err_scales, out):
    nc = tc.nc
    with ExitStack() as ctx:
        keep = ctx.enter_context(tc.tile_pool(name="keep", bufs=1))
        work = ctx.enter_context(tc.tile_pool(name="work", bufs=4))
        psum = ctx.enter_context(tc.psum_pool(name="psum", bufs=1))

        ident = keep.tile([P, P], F32, name="ident")
        identb = keep.tile([P, P], BF16, name="identb")
        lrow = keep.tile([P, 512], BF16, name="lrow", align_bytes=64)
        lcol = keep.tile([P, 4, SPK], BF16, name="lcol", align_bytes=64)
        lrep = keep.tile([P, 2, G, 2, 2, 64], BF16, name="lrep", align_bytes=64)
        dummy = keep.tile([P, 1], F32, name="dummy")
        xraw = [keep.tile([P, 4, D], BF16, name="xraw%d" % g) for g in range(G)]
        xcod = [keep.tile([P, 4, Q * P], U32, name="xcod%d" % g, align_bytes=64) for g in range(G)]
        xsca = [keep.tile([P, 4, Q * P], U8, name="xsca%d" % g, align_bytes=64) for g in range(G)]
        wraw = [[keep.tile([P, 4, WC], BF16, name="wraw%d_%d" % (c, q)) for q in range(Q)] for c in range(H // WC)]
        wcod = [[keep.tile([P, WC], U32, name="wcod%d_%d" % (c, q), align_bytes=64) for q in range(Q)] for c in range(H // WC)]
        wsca = [[keep.tile([P, WC], U8, name="wsca%d_%d" % (c, q), align_bytes=64) for q in range(Q)] for c in range(H // WC)]
        lraw = [keep.tile([P, G, 512], BF16, name="lraw%d" % c) for c in range(2)]
        amp = [keep.tile([P, G, 256], F32, name="amp%d" % c) for c in range(4)]
        hcod = [keep.tile([P, G, P], U32, name="hcod%d" % h, align_bytes=64) for h in range(NH)]
        hsca = [keep.tile([P, G, P], U8, name="hsca%d" % h, align_bytes=64) for h in range(NH)]
        ewor = [keep.tile([P, 2 * S], U8, name="ewor%d" % g, align_bytes=64) for g in range(G)]
        esca = keep.tile([P, G, S], U8, name="esca", align_bytes=64)

        def bank(i):
            b = psum.tile([P, 512], F32, name="bank%d" % i, tag="bank%d" % i)
            return b

        xbanks = [0, 1, 2, 3]
        zbanks = [4, 5, 6]
        obanks = [7, 1, 0, 3, 2]
        count = {"z": 0, "o": 0}

        def load_x(g, a, b):
            nc.sync.dma_start(out=xraw[g][:, a:b, :], in_=x[512 * g : 512 * (g + 1), :].rearrange("(m t) k -> m t k", t=4)[:, a:b, :])

        def load_w(c):
            for q in range(Q):
                nc.sync.dma_start(
                    out=wraw[c][q][:],
                    in_=w[512 * q : 512 * (q + 1), WC * c : WC * (c + 1)].rearrange("(p j) n -> p j n", j=4),
                )

        def load_lhuc(c, lo, hi):
            rows = lhuc.rearrange("(g s) n -> s g n", s=2)
            for s in range(2):
                nc.sync.dma_start(
                    out=lraw[c][64 * s : 64 * (s + 1), lo:hi, :],
                    in_=rows[s, lo:hi, 512 * c : 512 * (c + 1)].partition_broadcast(64),
                )

        def load_esca():
            for k in range(4):
                nc.sync.dma_start(
                    out=esca[32 * k : 32 * k + 4, :, :].bitcast(I32),
                    in_=err_scales[:, 4 * k : 4 * (k + 1), :].rearrange("g r n -> r g n").bitcast(I32),
                )

        def load_ewor(g):
            nc.sync.dma_start(out=ewor[g][:].bitcast(I32), in_=err_words[g].bitcast(I32))

        xgrp = {}
        xord = {}

        def xorder(g, t, eng):
            xo = work.tile([P, 512], F32, name="xo", tag="xo", bufs=6)
            dst = xo[:].rearrange("p (q u m) -> p q u m", q=Q, u=2)
            src = xraw[g][:, t, :].bitcast(F32).rearrange("p (q m u) -> p q u m", q=Q, u=2)
            if eng == "s":
                nc.scalar.copy(out=dst, in_=src)
            else:
                nc.vector.tensor_copy(out=dst, in_=src)
            xord[g, t] = xo

        def trans(g, t):
            b = bank(xbanks[t])
            words = xraw[g][:, t, :].bitcast(F32)
            for q in range(Q):
                for u in range(2):
                    j = 2 * q + u
                    if (g, t) in xord:
                        cols = xord[g, t][:, P * j : P * (j + 1)]
                    else:
                        cols = words[:, 256 * q + u : 256 * (q + 1) : 2]
                    nc.tensor.transpose(b[:, P * j : P * (j + 1)], cols, ident[:])
            xg = work.tile([P, Q, P, 4], BF16, name="xg", tag="xg", align_bytes=64)
            nc.scalar.copy(
                out=xg[:].rearrange("p q m t -> p (q m t)").bitcast(F32),
                in_=b[:].rearrange("p (q u m) -> p q m u", q=Q, u=2),
            )
            xgrp[g, t] = xg

        def xquant(g, t):
            nc.vector.quantize_mx(
                out=xcod[g][:, t, :].bitcast(FP8X4),
                scales=xsca[g][:, t, :],
                in_=xgrp[g, t][:].rearrange("p q m t -> p (q m t)"),
            )

        wgrp = {}

        def winter(h, q, eng, n=1):
            c, off = divmod(P * h, WC)
            wg = work.tile([P, P * n, 4], BF16, name="wg", tag="wg", align_bytes=64)
            src = wraw[c][q][:, :, off : off + P * n].rearrange("p j n -> p n j")
            if eng == "s":
                nc.scalar.copy(out=wg[:], in_=src)
            else:
                nc.vector.tensor_copy(out=wg[:], in_=src)
            wgrp[h, q] = wg

        def wquant(h, q, n=1):
            c, off = divmod(P * h, WC)
            nc.vector.quantize_mx(
                out=wcod[c][q][:, off : off + P * n].bitcast(FP8X4),
                scales=wsca[c][q][:, off : off + P * n],
                in_=wgrp[h, q][:].rearrange("p n j -> p (n j)"),
            )

        def lhuc_turn():
            b = psum.tile([P, 4, P], BF16, name="bank5l", tag="bank5")
            for h in range(4):
                nc.tensor.transpose(b[:, h, :], lrow[:, P * h : P * (h + 1)], identb[:])
            nc.vector.tensor_copy(out=lcol[:], in_=b[:, :, 0:SPK])

        def lhuc_repeat(a, g, eng):
            src = lcol[:, 2 * a : 2 * (a + 1), 2 * g : 2 * (g + 1)].unsqueeze(3).to_broadcast([P, 2, 2, 64])
            if eng == "s":
                nc.scalar.copy(out=lrep[:, a, g, :, :, :], in_=src)
            else:
                nc.vector.tensor_copy(out=lrep[:, a, g, :, :, :], in_=src)

        def lhuc_spread(a, lo, hi, i):
            b = psum.tile([P, G, 256], BF16, name="bank%dl" % i, tag="bank%d" % i)
            for g in range(lo, hi):
                for h in range(2):
                    nc.tensor.transpose(
                        b[:, g, P * h : P * (h + 1)], lrep[:, a, g, h, :, :].rearrange("p s r -> p (s r)"), identb[:]
                    )
            nc.scalar.activation(out=amp[a][:, lo:hi, :], in_=b[:, lo:hi, :], func=ACT.Sigmoid)

        def sigm(c, lo, hi):
            nc.scalar.activation(out=amp[c][:, lo:hi, :], in_=lraw[c // 2][:, lo:hi, 256 * (c % 2) : 256 * (c % 2 + 1)], func=ACT.Sigmoid)

        zb = {}
        hgrp = {}

        def s1(g, h):
            z = bank(zbanks[count["z"] % len(zbanks)])
            count["z"] += 1
            c, off = divmod(P * h, WC)
            for t in range(4):
                for q in range(Q):
                    nc.tensor.matmul_mx(
                        out=z[:, P * t : P * (t + 1)],
                        lhsT=xcod[g][:, t, P * q : P * (q + 1)].bitcast(FP8X4),
                        lhsT_scale=xsca[g][:, t, P * q : P * (q + 1)],
                        rhs=wcod[c][q][:, off : off + P].bitcast(FP8X4),
                        rhs_scale=wsca[c][q][:, off : off + P],
                        start=(q == 0),
                        stop=(q == Q - 1),
                    )
            zb[g, h] = z

        def hevict(g, h):
            c, off = divmod(P * h, 256)
            hg = work.tile([P, P, 4], BF16, name="hg", tag="hg", align_bytes=64)
            nc.vector.scalar_tensor_tensor(
                out=hg[:],
                in0=zb[g, h][:].rearrange("p (t n) -> p n t", t=4),
                scalar=0.0,
                in1=amp[c][:, g, off : off + P].unsqueeze(2).to_broadcast([P, P, 4]),
                op0=ALU.max,
                op1=ALU.mult,
            )
            hgrp[g, h] = hg

        def hquant(g, h):
            nc.vector.quantize_mx(
                out=hcod[h][:, g, :].bitcast(FP8X4),
                scales=hsca[h][:, g, :],
                in_=hgrp[g, h][:].rearrange("p n t -> p (n t)"),
            )

        pend = []

        def s1h(g, h):
            s1(g, h)
            hevict(g, h)
            if pend:
                hquant(*pend.pop())
            pend.append((g, h))

        def flush():
            if pend:
                hquant(*pend.pop())

        ob = {}
        og = {}

        def s2(h, n, groups):
            if groups[0] == 0:
                ob[h, n] = bank(obanks[count["o"] % len(obanks)])
                count["o"] += 1
            for g in groups:
                nc.tensor.matmul_mx(
                    out=ob[h, n][:],
                    lhsT=hcod[h][:, g, :].bitcast(FP8X4),
                    lhsT_scale=hsca[h][:, g, :],
                    rhs=ewor[g][:, 1024 * n : 1024 * (n + 1)].bitcast(FP4X4),
                    rhs_scale=esca[:, g, 512 * n : 512 * (n + 1)],
                    start=(g == 0),
                    stop=(g == G - 1),
                )

        def oevict(h, n, eng, lo=0, hi=512):
            if h not in og:
                og[h] = work.tile([P, S], F32, name="og", tag="og", bufs=3)
            dst = og[h][:, 512 * n + lo : 512 * n + hi]
            src = ob[h, n][:, lo:hi]
            if eng == "s":
                nc.scalar.activation(out=dst, in_=src, func=ACT.Copy, scale=2.0)
            else:
                nc.vector.tensor_scalar(out=dst, in0=src, scalar1=2.0, scalar2=None, op0=ALU.mult)

        def store(h, lo, hi):
            nc.sync.dma_start(out=out[P * h : P * (h + 1), lo:hi], in_=og[h][:, lo:hi])

        with tc.manual_schedule():
            nc.vector.memset(dummy[:], 0.0)
            nc.vector.memset(lrow[:], 0.0)
            nc.scalar.dma_start(out=lrow[0:SPK, :], in_=lhuc[:, 0:512])
            nc.scalar.activation(out=dummy[:], in_=dummy[:], func=ACT.Sigmoid)
            make_identity(nc, ident[:])
            make_identity(nc, identb[:])
            nc.vector.memset(esca[:].rearrange("p g n -> p (g n)").bitcast(I32), 0)
            load_x(0, 0, 1)
            load_x(0, 1, 2)
            load_x(0, 2, 3)
            load_x(0, 3, 4)
            load_w(0)
            load_x(1, 0, 2)
            load_x(1, 2, 4)
            load_x(2, 0, 4)
            load_x(3, 0, 4)
            load_w(1)
            load_esca()
            for g in range(G):
                load_ewor(g)
            load_w(2)
            load_w(3)
            load_lhuc(1, 0, 4)

            trans(0, 0)
            trans(0, 1)
            lhuc_turn()
            lhuc_repeat(0, 0, "v")
            trans(0, 2)
            trans(0, 3)
            xquant(0, 0)
            xquant(0, 1)
            winter(0, 0, "v")
            winter(0, 1, "v")
            xquant(0, 2)
            wquant(0, 0)
            wquant(0, 1)
            xquant(0, 3)
            lhuc_spread(0, 0, 1, 7)
            winter(1, 0, "s")
            winter(1, 1, "v")
            lhuc_repeat(0, 1, "v")
            wquant(1, 1)
            wquant(1, 0)
            lhuc_repeat(0, 2, "v")
            lhuc_repeat(0, 3, "v")
            s1h(0, 0)
            trans(1, 0)
            xquant(1, 0)
            trans(1, 1)
            xquant(1, 1)
            xorder(2, 0, "v")
            trans(1, 2)
            xquant(1, 2)
            xorder(2, 1, "v")
            trans(1, 3)
            xquant(1, 3)
            xorder(2, 2, "v")
            xorder(2, 3, "v")
            lhuc_spread(0, 1, 4, 6)
            s1h(0, 1)
            for t in range(4):
                trans(2, t)
                xquant(2, t)
                if t % 2:
                    xorder(3, t, "v")
            xorder(3, 0, "s")
            s1h(1, 0)
            s1h(1, 1)
            for t in (1, 0, 3, 2):
                trans(3, t)
                xquant(3, t)
            s1h(2, 0)
            winter(2, 0, "s")
            s1h(2, 1)
            for g in (0, 1):
                for n in range(NS):
                    s2(0, n, [g])
            winter(2, 1, "s")
            for g in range(G):
                lhuc_repeat(1, g, "s")
            wquant(2, 0)
            wquant(2, 1)
            s1h(3, 0)
            s1h(3, 1)
            flush()
            lhuc_spread(1, 0, 4, 3)
            winter(3, 0, "s")
            winter(3, 1, "v")
            wquant(3, 0)
            wquant(3, 1)
            for h in range(NH):
                z = h + 2
                if z < NH:
                    s1h(0, z)
                if z == 3:
                    winter(4, 0, "s", 2)
                    winter(4, 1, "s", 2)
                    sigm(2, 0, 4)
                    wquant(4, 0, 2)
                    wquant(4, 1, 2)
                if z == 5:
                    sigm(3, 0, 4)
                    winter(6, 0, "s", 2)
                    winter(6, 1, "s", 2)
                    wquant(6, 0, 2)
                    wquant(6, 1, 2)
                for n in range(NS):
                    s2(h, n, [2, 3] if h == 0 else [0, 1, 2, 3])
                    if h < NH - 1:
                        oevict(h, n, "s")
                    elif n < NS - 1:
                        oevict(h, n, "sv"[n])
                        store(h, 512 * n, 512 * (n + 1))
                    else:
                        oevict(h, n, "s", 0, 256)
                        oevict(h, n, "v", 256, 512)
                        store(h, 512 * n, 512 * (n + 1))
                    if z < NH:
                        s1h(n + 1, z)
                if h < NH - 1:
                    store(h, 0, S)
                if z == NH - 1:
                    flush()
